import numpy as np
import ml_dtypes


def mxq(x, axis, fmt="e4m3"):
    dtype, down = {"e4m3": (ml_dtypes.float8_e4m3fn, 7), "e5m2": (ml_dtypes.float8_e5m2, 14)}[fmt]
    v = np.moveaxis(np.asarray(x, np.float32).astype(ml_dtypes.bfloat16).astype(np.float64), axis, -1)
    blocks = v.reshape(v.shape[:-1] + (-1, 32))
    amax = np.abs(blocks).max(-1, keepdims=True)
    byte = np.maximum(np.where(amax > 0, np.frexp(amax)[1] - 1 + 127, 0) - down, 1)
    scale = np.exp2(byte - 127.0)
    codes = (blocks / scale).astype(np.float32).astype(dtype).astype(np.float64)
    return np.moveaxis((codes * scale).reshape(v.shape), -1, axis)


WIDE = False


def mx_kscale(k):
    if not WIDE:
        return np.ones(k)
    levels = np.array([10, -10, 5, -5, 0])
    if k % 512:
        return np.exp2(np.random.permutation(np.resize(levels, k // 32))).repeat(32)
    a = np.empty((k // 512, 16))
    for p in range(k // 512):
        a[p, :8] = np.random.permutation(np.resize(levels, 8))
        for g in range(8):
            far = levels[np.abs(levels - a[p, g]) >= 10]
            a[p, g + 8] = far[np.random.randint(len(far))]
    return np.exp2(a.ravel()).repeat(32)


def f64(x):
    return np.asarray(x).astype(np.float64)


def striped(idx):
    return np.tile(np.asarray(idx).reshape(-1, 16).T, (8, 1)).astype(np.uint16)


def unstriped(offs):
    return offs[:16].T.reshape(-1).astype(np.int64)


E2M1 = np.array([0.0, 0.5, 1.0, 1.5, 2.0, 3.0, 4.0, 6.0, -0.0, -0.5, -1.0, -1.5, -2.0, -3.0, -4.0, -6.0])


def pack_weight(w, fmt):
    k, n = w.shape
    w = f64(np.asarray(w, np.float32).astype(ml_dtypes.bfloat16)).reshape(k // 32, 32, n)
    amax = np.abs(w).max(1)
    if fmt == "e4m3":
        byte = np.frexp(amax)[1] - 1 + 127 - 7
    else:
        mant, ex = np.frexp(amax / 6.0)
        byte = np.where(mant > 0.5, ex, ex - 1) + 127
    byte = np.clip(np.where(amax > 0, byte, 1), 1, 254)
    scaled = (w * np.exp2(127.0 - byte)[:, None, :]).reshape(k, n).astype(np.float32)
    by_word = np.ascontiguousarray(scaled.reshape(k // 512, 128, 4, n).transpose(0, 1, 3, 2))
    if fmt == "e4m3":
        words = by_word.astype(ml_dtypes.float8_e4m3fn).view(np.uint8)
    else:
        c = by_word.astype(ml_dtypes.float4_e2m1fn).view(np.uint8) & 0xF
        words = (c[..., 0::2] | (c[..., 1::2] << 4)).reshape(k // 512, 128, 2 * n)
    return np.ascontiguousarray(words), np.ascontiguousarray(byte.astype(np.uint8).reshape(k // 512, 16, n))


def unpack_weight(words, scales, fmt):
    g, _, n = scales.shape
    words = np.ascontiguousarray(words).reshape(g, 128, n, -1)
    if fmt == "e4m3":
        vals = words.view(ml_dtypes.float8_e4m3fn).astype(np.float64)
    else:
        nib = np.empty((g, 128, n, 4), np.uint8)
        nib[..., 0::2] = words & 0xF
        nib[..., 1::2] = words >> 4
        vals = E2M1[nib]
    vals = vals * np.repeat(np.exp2(scales.astype(np.float64) - 127.0), 8, axis=1)[..., None]
    return vals.transpose(0, 1, 3, 2).reshape(g * 512, n)


def rot(x):
    y = x.reshape(-1, 2, x.shape[1])
    return np.stack([-y[:, 1], y[:, 0]], axis=1).reshape(x.shape)


D, T, I, U, V, Q = 512, 1024, 256, 512, 1024, 256


def setup_inputs():
    n = np.random.standard_normal
    idx = np.random.permutation(T)[:I]
    idx2 = np.random.permutation(T)[:I]
    idx3 = np.random.randint(0, U, I)
    idx4 = np.random.permutation(V)[:Q]
    fd = mx_kscale(D)
    queryp = pack_weight(n((D, V)) * 0.7 / np.sqrt(D) * fd[:, None], "e4m3")
    return {
        "query_words": queryp[0],
        "query_scales": queryp[1],
        "keys": (n((D, T)) / fd[:, None]).astype(np.float32),
        "cosn": (np.repeat(np.round(np.cos(np.arange(D // 2)[:, None] * 0.11 + np.arange(U)[None] * 0.37) * 64) / 64, 2, axis=0)).astype(np.float32),
        "sinn": (np.repeat(np.round(np.sin(np.arange(D // 2)[:, None] * 0.11 + np.arange(U)[None] * 0.37) * 64) / 64, 2, axis=0)).astype(np.float32),
        "kept": (n((D, T)) * 0.7 / fd[:, None]).astype(np.float32),
        "offs": striped(idx),
        "offs2": striped(idx2),
        "offs3": striped(idx3),
        "offs4": striped(idx4),
    }


def reference(query_words, query_scales, keys, cosn, sinn, kept, offs, offs2, offs3, offs4):
    idx = unstriped(offs)
    idx2 = unstriped(offs2)
    idx3 = unstriped(offs3)
    idx4 = unstriped(offs4)
    queryu = unpack_weight(query_words, query_scales, "e4m3")
    kr = rot(f64(keys)[:, idx])
    kt = f64(keys)[:, idx] * f64(cosn)[:, idx3] + kr * f64(sinn)[:, idx3]
    kf = np.zeros((D, T))
    kf[:, idx2] = kt
    kn = kf + f64(kept)
    queryidx4g = queryu[:, idx4]
    knq = mxq(kn, 0, "e4m3")
    a = queryidx4g.T @ knq
    p = np.exp(a - np.max(a, axis=1, keepdims=True))
    y = p / np.sum(p, axis=1, keepdims=True) * 512.0
    return y

@@ -1,0 +1,193 @@
+from contextlib import ExitStack
+
+import concourse.mybir as mybir
+from concourse.masks import make_identity
+
+D, T, I, U, V, Q = 512, 1024, 256, 512, 1024, 256
+FLOPS = 2 * Q * T * D
+
+F32 = mybir.dt.float32
+BF16 = mybir.dt.bfloat16
+I32 = mybir.dt.int32
+U32 = mybir.dt.uint32
+U16 = mybir.dt.uint16
+U8 = mybir.dt.uint8
+FP8X4 = mybir.dt.float8_e4m3fn_x4
+ALU = mybir.AluOpType
+ACT = mybir.ActivationFunctionType
+AX = mybir.AxisListType
+
+P = 128
+CH = 256
+NCH = T // CH
+HALF = 512
+
+
+def tile_attend_turnedkeys_kernel(tc, query_words, query_scales, keys, cosn, sinn, kept, offs, offs2, offs3, offs4, out):
+    nc = tc.nc
+    with ExitStack() as ctx:
+        lists = ctx.enter_context(tc.tile_pool(name="lists", bufs=1))
+        sb = ctx.enter_context(tc.tile_pool(name="sb", bufs=1))
+        ps = ctx.enter_context(tc.psum_pool(name="ps", bufs=1))
+
+        o_key = lists.tile([P, I // 16], U16, name="o_key")
+        o_place = lists.tile([P, I // 16], U16, name="o_place")
+        o_dist = lists.tile([P, I // 16], U16, name="o_dist")
+        o_query = lists.tile([P, Q // 16], U16, name="o_query")
+
+        keys_r = keys.rearrange("(p r) t -> p r t", r=4)
+        kept_r = kept.rearrange("(p r) t -> p r t", r=4)
+        cos_r = cosn.rearrange("(p r) u -> p r u", r=4)
+        sin_r = sinn.rearrange("(p r) u -> p r u", r=4)
+
+        key_t = [sb.tile([P, T], F32, name=f"key{r}") for r in range(4)]
+        kept_t = [sb.tile([P, T], F32, name=f"kept{r}") for r in range(4)]
+        kf_t = [sb.tile([P, T], F32, name=f"kf{r}") for r in range(4)]
+        cos_t = [sb.tile([P, U], F32, name=f"cos{u}") for u in range(2)]
+        sin_t = [sb.tile([P, U], F32, name=f"sin{u}") for u in range(2)]
+        qw = sb.tile([P, V], U32, name="qw")
+        qs = sb.tile([P, V], U8, name="qs")
+        ident = sb.tile([P, P], F32, name="ident")
+
+        nc.vector.memset(qs[:].bitcast(I32), 0)
+        for r in range(2):
+            nc.vector.memset(kf_t[r][:].bitcast(I32), 0)
+        make_identity(nc, ident[:])
+        for r in range(2, 4):
+            nc.gpsimd.memset(kf_t[r][:].bitcast(I32), 0)
+
+        nc.sync.dma_start(o_dist[:], offs3)
+        nc.sync.dma_start(cos_t[0][:], cos_r[:, 0, :])
+        nc.sync.dma_start(sin_t[0][:], sin_r[:, 0, :])
+        nc.sync.dma_start(o_key[:], offs)
+        nc.sync.dma_start(key_t[0][:], keys_r[:, 0, :])
+        nc.sync.dma_start(key_t[1][:], keys_r[:, 1, :])
+        nc.sync.dma_start(o_place[:], offs2)
+        nc.sync.dma_start(o_query[:], offs4)
+        qs_rows = query_scales[0].bitcast(I32)
+        for g in range(4):
+            nc.sync.dma_start(qs[:].bitcast(I32)[32 * g:32 * g + 4, :], qs_rows[4 * g:4 * g + 4, :])
+        nc.sync.dma_start(kept_t[0][:], kept_r[:, 0, :])
+        nc.sync.dma_start(kept_t[1][:], kept_r[:, 1, :])
+        nc.sync.dma_start(cos_t[1][:], cos_r[:, 2, :])
+        nc.sync.dma_start(sin_t[1][:], sin_r[:, 2, :])
+        nc.sync.dma_start(key_t[2][:], keys_r[:, 2, :])
+        nc.sync.dma_start(key_t[3][:], keys_r[:, 3, :])
+        nc.sync.dma_start(kept_t[2][:], kept_r[:, 2, :])
+        nc.sync.dma_start(kept_t[3][:], kept_r[:, 3, :])
+        nc.sync.dma_start(qw[:].bitcast(I32), query_words[0].rearrange("p n t -> p (n t)").bitcast(I32))
+
+        qwg = sb.tile([P, Q], U32, name="qwg", align_bytes=64)
+        qsg = sb.tile([P, Q], U8, name="qsg", align_bytes=64)
+
+        def rotate_and_scatter(u):
+            trig = sb.tile([P, 3, I], F32, name=f"trig{u}")
+            kg = [sb.tile([P, I], F32, name=f"kg{u}_{e}") for e in range(2)]
+            prod = [sb.tile([P, 2, I], F32, name=f"prod{u}_{e}") for e in range(2)]
+            nc.vector.tensor_copy(trig[:, 1, :], cos_t[u][:].indirect(o_dist[:]))
+            nc.vector.tensor_copy(trig[:, 0, :], sin_t[u][:].indirect(o_dist[:]))
+            nc.scalar.mul(trig[:, 2, :], trig[:, 0, :], -1.0)
+            if u == 0:
+                nc.vector.tensor_copy(qsg[:], qs[:].indirect(o_query[:]))
+            for e in range(2):
+                nc.vector.tensor_copy(kg[e][:], key_t[2 * u + e][:].indirect(o_key[:]))
+            for e in range(2):
+                nc.vector.tensor_tensor(prod[e][:], kg[e][:].unsqueeze(1).to_broadcast([P, 2, I]), trig[:, e:e + 2, :], ALU.mult)
+            for e in range(2):
+                nc.vector.tensor_tensor(kf_t[2 * u + e][:].indirect(o_place[:]), prod[0][:, 1 - e, :], prod[1][:, 1 - e, :], ALU.add)
+
+        def add_turned(u, banks):
+            for src, first in ((kept_t, True), (kf_t, False)):
+                for e in range(2):
+                    for c in range(NCH):
+                        for j in range(2):
+                            t0 = c * CH + j * P
+                            nc.tensor.matmul(
+                                banks[c][:, j, e, :], src[2 * u + e][:, t0:t0 + P], ident[:],
+                                start=(first and e == 0 and j == 0),
+                                stop=((not first) and e == 1 and j == 1),
+                                is_transpose=True,
+                            )
+
+        def round_pairs(u, c, bank, on_vector):
+            w = sb.tile([P, 2, P, 2], BF16, name=f"w{u}_{c}")
+            src = bank[:].rearrange("t j e p -> t j p e")
+            if on_vector:
+                nc.vector.tensor_copy(w[:], src)
+            else:
+                nc.scalar.copy(w[:], src)
+            return w
+
+        def turn_back(u, w, bank):
+            words = w[:].rearrange("t j p e -> t (j p e)").bitcast(F32)
+            for j in range(2):
+                nc.tensor.transpose(bank[:, u, j * P:(j + 1) * P], words[:, j * P:(j + 1) * P], ident[:])
+
+        banks0 = [ps.tile([P, 2, 2, P], F32, name=f"sum0_{c}", tag=f"a{c}") for c in range(NCH)]
+        banks1 = [ps.tile([P, 2, 2, P], F32, name=f"sum1_{c}", tag=f"b{c}") for c in range(NCH)]
+
+        rotate_and_scatter(0)
+        add_turned(0, banks0)
+        w0 = [round_pairs(0, c, banks0[c], False) for c in range(NCH)]
+        back = [ps.tile([P, 2, CH], F32, name=f"back{c}", tag=f"a{c}") for c in range(NCH)]
+        rotate_and_scatter(1)
+        nc.vector.tensor_copy(qwg[:], qw[:].indirect(o_query[:]))
+        for c in range(NCH):
+            turn_back(0, w0[c], back[c])
+        add_turned(1, banks1)
+        w1 = [round_pairs(1, c, banks1[c], c % 2 == 1) for c in range(NCH)]
+        for c in range(NCH):
+            turn_back(1, w1[c], back[c])
+
+        pieces = [(0, 2, ("b0", "b1")), (2, 1, ("b2", "b3")), (3, 1, ("a0", "a1"))]
+        npc = len(pieces)
+        nmax = [sb.tile([P, npc], F32, name=f"nmax{m}") for m in range(2)]
+        sums = [sb.tile([P, npc], F32, name=f"sums{m}") for m in range(2)]
+        ex = [sb.tile([P, T], F32, name=f"ex{m}") for m in range(2)]
+        quant = []
+        for c in range(NCH):
+            knb = sb.tile([P, CH * 4], BF16, name=f"knb{c}", align_bytes=64)
+            dst = knb[:].bitcast(F32).rearrange("p (t u) -> p t u", u=2)
+            src = back[c][:].rearrange("p u t -> p t u")
+            if c == 1:
+                nc.vector.tensor_copy(dst, src)
+            else:
+                nc.scalar.copy(dst, src)
+            codes = sb.tile([P, CH], U32, name=f"codes{c}", align_bytes=64)
+            scales = sb.tile([P, CH], U8, name=f"scales{c}", align_bytes=64)
+            nc.vector.quantize_mx(out=codes[:].bitcast(FP8X4), scales=scales[:], in_=knb[:])
+            quant.append((codes, scales))
+
+        for k, (c0, n, tags) in enumerate(pieces):
+            score = [ps.tile([P, n * CH], F32, name=f"score{k}_{m}", tag=tags[m]) for m in range(2)]
+            for c in range(c0, c0 + n):
+                for m in range(2):
+                    nc.tensor.matmul_mx(
+                        out=score[m][:, (c - c0) * CH:(c - c0 + 1) * CH],
+                        lhsT=qwg[:, m * P:(m + 1) * P].bitcast(FP8X4),
+                        lhsT_scale=qsg[:, m * P:(m + 1) * P],
+                        rhs=quant[c][0][:].bitcast(FP8X4),
+                        rhs_scale=quant[c][1][:],
+                        start=True, stop=True,
+                    )
+            for m in range(2):
+                nc.vector.tensor_reduce(nmax[m][:, k:k + 1], score[m][:], AX.X, ALU.max, negate=True)
+                nc.scalar.activation(ex[m][:, c0 * CH:(c0 + n) * CH], score[m][:], ACT.Exp, bias=nmax[m][:, k:k + 1], accum_out=sums[m][:, k:k + 1])
+
+        for m in range(2):
+            nall = sb.tile([P, 1], F32, name=f"nall{m}")
+            fac = sb.tile([P, npc], F32, name=f"fac{m}")
+            terms = sb.tile([P, npc], F32, name=f"terms{m}")
+            total = sb.tile([P, 1], F32, name=f"total{m}")
+            inv = sb.tile([P, 1], F32, name=f"inv{m}")
+            res = sb.tile([P, T], F32, name=f"res{m}")
+            nc.vector.tensor_reduce(nall[:], nmax[m][:], AX.X, ALU.min)
+            nc.scalar.activation(fac[:], nmax[m][:], ACT.Exp, bias=nall[:], scale=-1.0)
+            nc.vector.scalar_tensor_tensor(terms[:], fac[:], 1.0 / 512.0, sums[m][:], ALU.mult, ALU.mult, accum_out=total[:])
+            nc.vector.reciprocal(inv[:], total[:])
+            for k, (c0, n, tags) in enumerate(pieces):
+                cols = slice(c0 * CH, (c0 + n) * CH)
+                nc.vector.tensor_scalar(res[:, cols], ex[m][:, cols], fac[:, k:k + 1], inv[:], ALU.mult, ALU.mult)
+                if (c0 + n) % 2 == 0:
+                    half = slice((c0 + n) * CH - HALF, (c0 + n) * CH)
+                    nc.sync.dma_start(out[m * P:(m + 1) * P, half], res[:, half])

@@ -40,7 +40,10 @@ def tile_attend_turnedkeys_kernel(tc, query_words, query_scales, keys, cosn, sin
         cos_r = cosn.rearrange("(p r) u -> p r u", r=4)
         sin_r = sinn.rearrange("(p r) u -> p r u", r=4)
 
-        key_t = [sb.tile([P, T], F32, name=f"key{r}") for r in range(4)]
+        key0 = sb.tile([P, T], F32, name="key0")
+        key1 = sb.tile([P, T], F32, name="key1")
+        key23 = sb.tile([P, 2 * T], F32, name="key23")
+        key_w = [key0[:], key1[:], key23[:, 0:T], key23[:, T:2 * T]]
         kept_t = [sb.tile([P, T], F32, name=f"kept{r}") for r in range(4)]
         kf_t = [sb.tile([P, T], F32, name=f"kf{r}") for r in range(4)]
         cos_t = [sb.tile([P, U], F32, name=f"cos{u}") for u in range(2)]
@@ -49,10 +52,10 @@ def tile_attend_turnedkeys_kernel(tc, query_words, query_scales, keys, cosn, sin
         qs = sb.tile([P, V], U8, name="qs")
         ident = sb.tile([P, P], F32, name="ident")
 
-        nc.vector.memset(qs[:].bitcast(I32), 0)
         for r in range(2):
             nc.vector.memset(kf_t[r][:].bitcast(I32), 0)
         make_identity(nc, ident[:])
+        nc.gpsimd.memset(qs[:].bitcast(I32), 0)
         for r in range(2, 4):
             nc.gpsimd.memset(kf_t[r][:].bitcast(I32), 0)
 
@@ -60,22 +63,21 @@ def tile_attend_turnedkeys_kernel(tc, query_words, query_scales, keys, cosn, sin
         nc.sync.dma_start(cos_t[0][:], cos_r[:, 0, :])
         nc.sync.dma_start(sin_t[0][:], sin_r[:, 0, :])
         nc.sync.dma_start(o_key[:], offs)
-        nc.sync.dma_start(key_t[0][:], keys_r[:, 0, :])
-        nc.sync.dma_start(key_t[1][:], keys_r[:, 1, :])
+        nc.sync.dma_start(key0[:], keys_r[:, 0, :])
+        nc.sync.dma_start(cos_t[1][:], cos_r[:, 2, :])
+        nc.sync.dma_start(key1[:], keys_r[:, 1, :])
+        nc.sync.dma_start(sin_t[1][:], sin_r[:, 2, :])
         nc.sync.dma_start(o_place[:], offs2)
+        nc.sync.dma_start(kept_t[0][:], kept_r[:, 0, :])
+        nc.sync.dma_start(kept_t[1][:], kept_r[:, 1, :])
+        nc.sync.dma_start(key23[:], keys.rearrange("(p g r) t -> p g (r t)", g=2, r=2)[:, 1, :])
+        nc.sync.dma_start(kept_t[2][:], kept_r[:, 2, :])
+        nc.sync.dma_start(kept_t[3][:], kept_r[:, 3, :])
+        nc.sync.dma_start(qw[:].bitcast(I32), query_words[0].rearrange("p n t -> p (n t)").bitcast(I32))
         nc.sync.dma_start(o_query[:], offs4)
         qs_rows = query_scales[0].bitcast(I32)
         for g in range(4):
             nc.sync.dma_start(qs[:].bitcast(I32)[32 * g:32 * g + 4, :], qs_rows[4 * g:4 * g + 4, :])
-        nc.sync.dma_start(kept_t[0][:], kept_r[:, 0, :])
-        nc.sync.dma_start(kept_t[1][:], kept_r[:, 1, :])
-        nc.sync.dma_start(cos_t[1][:], cos_r[:, 2, :])
-        nc.sync.dma_start(sin_t[1][:], sin_r[:, 2, :])
-        nc.sync.dma_start(key_t[2][:], keys_r[:, 2, :])
-        nc.sync.dma_start(key_t[3][:], keys_r[:, 3, :])
-        nc.sync.dma_start(kept_t[2][:], kept_r[:, 2, :])
-        nc.sync.dma_start(kept_t[3][:], kept_r[:, 3, :])
-        nc.sync.dma_start(qw[:].bitcast(I32), query_words[0].rearrange("p n t -> p (n t)").bitcast(I32))
 
         qwg = sb.tile([P, Q], U32, name="qwg", align_bytes=64)
         qsg = sb.tile([P, Q], U8, name="qsg", align_bytes=64)
@@ -87,10 +89,8 @@ def tile_attend_turnedkeys_kernel(tc, query_words, query_scales, keys, cosn, sin
             nc.vector.tensor_copy(trig[:, 1, :], cos_t[u][:].indirect(o_dist[:]))
             nc.vector.tensor_copy(trig[:, 0, :], sin_t[u][:].indirect(o_dist[:]))
             nc.scalar.mul(trig[:, 2, :], trig[:, 0, :], -1.0)
-            if u == 0:
-                nc.vector.tensor_copy(qsg[:], qs[:].indirect(o_query[:]))
             for e in range(2):
-                nc.vector.tensor_copy(kg[e][:], key_t[2 * u + e][:].indirect(o_key[:]))
+                nc.vector.tensor_copy(kg[e][:], key_w[2 * u + e].indirect(o_key[:]))
             for e in range(2):
                 nc.vector.tensor_tensor(prod[e][:], kg[e][:].unsqueeze(1).to_broadcast([P, 2, I]), trig[:, e:e + 2, :], ALU.mult)
             for e in range(2):
@@ -132,62 +132,65 @@ def tile_attend_turnedkeys_kernel(tc, query_words, query_scales, keys, cosn, sin
         back = [ps.tile([P, 2, CH], F32, name=f"back{c}", tag=f"a{c}") for c in range(NCH)]
         rotate_and_scatter(1)
         nc.vector.tensor_copy(qwg[:], qw[:].indirect(o_query[:]))
+        nc.vector.tensor_copy(qsg[:], qs[:].indirect(o_query[:]))
         for c in range(NCH):
             turn_back(0, w0[c], back[c])
         add_turned(1, banks1)
-        w1 = [round_pairs(1, c, banks1[c], c % 2 == 1) for c in range(NCH)]
+        w1 = [round_pairs(1, c, banks1[c], c >= 2) for c in range(NCH)]
         for c in range(NCH):
             turn_back(1, w1[c], back[c])
 
-        pieces = [(0, 2, ("b0", "b1")), (2, 1, ("b2", "b3")), (3, 1, ("a0", "a1"))]
-        npc = len(pieces)
-        nmax = [sb.tile([P, npc], F32, name=f"nmax{m}") for m in range(2)]
-        sums = [sb.tile([P, npc], F32, name=f"sums{m}") for m in range(2)]
+        pieces = [
+            [(0, 1, "b0"), (1, 1, "b2"), (2, 1, "a0"), (3, 1, "a2")],
+            [(0, 2, "b1"), (2, 1, "a1"), (3, 1, "a3")],
+        ]
+        nmax = [sb.tile([P, len(pieces[m])], F32, name=f"nmax{m}") for m in range(2)]
+        sums = [sb.tile([P, len(pieces[m])], F32, name=f"sums{m}") for m in range(2)]
         ex = [sb.tile([P, T], F32, name=f"ex{m}") for m in range(2)]
         quant = []
         for c in range(NCH):
             knb = sb.tile([P, CH * 4], BF16, name=f"knb{c}", align_bytes=64)
             dst = knb[:].bitcast(F32).rearrange("p (t u) -> p t u", u=2)
             src = back[c][:].rearrange("p u t -> p t u")
-            if c == 1:
-                nc.vector.tensor_copy(dst, src)
-            else:
-                nc.scalar.copy(dst, src)
+            nc.scalar.copy(dst, src)
             codes = sb.tile([P, CH], U32, name=f"codes{c}", align_bytes=64)
             scales = sb.tile([P, CH], U8, name=f"scales{c}", align_bytes=64)
             nc.vector.quantize_mx(out=codes[:].bitcast(FP8X4), scales=scales[:], in_=knb[:])
             quant.append((codes, scales))
 
-        for k, (c0, n, tags) in enumerate(pieces):
-            score = [ps.tile([P, n * CH], F32, name=f"score{k}_{m}", tag=tags[m]) for m in range(2)]
-            for c in range(c0, c0 + n):
-                for m in range(2):
-                    nc.tensor.matmul_mx(
-                        out=score[m][:, (c - c0) * CH:(c - c0 + 1) * CH],
-                        lhsT=qwg[:, m * P:(m + 1) * P].bitcast(FP8X4),
-                        lhsT_scale=qsg[:, m * P:(m + 1) * P],
-                        rhs=quant[c][0][:].bitcast(FP8X4),
-                        rhs_scale=quant[c][1][:],
-                        start=True, stop=True,
-                    )
+        score = [[ps.tile([P, n * CH], F32, name=f"score{m}_{c0}", tag=tag) for c0, n, tag in pieces[m]] for m in range(2)]
+        for c in range(NCH):
             for m in range(2):
-                nc.vector.tensor_reduce(nmax[m][:, k:k + 1], score[m][:], AX.X, ALU.max, negate=True)
-                nc.scalar.activation(ex[m][:, c0 * CH:(c0 + n) * CH], score[m][:], ACT.Exp, bias=nmax[m][:, k:k + 1], accum_out=sums[m][:, k:k + 1])
+                for k, (c0, n, tag) in enumerate(pieces[m]):
+                    if c0 <= c < c0 + n:
+                        nc.tensor.matmul_mx(
+                            out=score[m][k][:, (c - c0) * CH:(c - c0 + 1) * CH],
+                            lhsT=qwg[:, m * P:(m + 1) * P].bitcast(FP8X4),
+                            lhsT_scale=qsg[:, m * P:(m + 1) * P],
+                            rhs=quant[c][0][:].bitcast(FP8X4),
+                            rhs_scale=quant[c][1][:],
+                            start=True, stop=True,
+                        )
+
+        fac = [sb.tile([P, len(pieces[m])], F32, name=f"fac{m}") for m in range(2)]
+        inv = [sb.tile([P, 1], F32, name=f"inv{m}") for m in range(2)]
+        for m in range(2):
+            for k, (c0, n, tag) in enumerate(pieces[m]):
+                nc.vector.tensor_reduce(nmax[m][:, k:k + 1], score[m][k][:], AX.X, ALU.max, negate=True)
+                nc.scalar.activation(ex[m][:, c0 * CH:(c0 + n) * CH], score[m][k][:], ACT.Exp, bias=nmax[m][:, k:k + 1], accum_out=sums[m][:, k:k + 1])
+            nall = sb.tile([P, 1], F32, name=f"nall{m}")
+            terms = sb.tile([P, len(pieces[m])], F32, name=f"terms{m}")
+            total = sb.tile([P, 1], F32, name=f"total{m}")
+            nc.vector.tensor_reduce(nall[:], nmax[m][:], AX.X, ALU.min)
+            nc.scalar.activation(fac[m][:], nmax[m][:], ACT.Exp, bias=nall[:], scale=-1.0)
+            nc.vector.scalar_tensor_tensor(terms[:], fac[m][:], 1.0 / 512.0, sums[m][:], ALU.mult, ALU.mult, accum_out=total[:])
+            nc.vector.reciprocal(inv[m][:], total[:])
 
         for m in range(2):
-            nall = sb.tile([P, 1], F32, name=f"nall{m}")
-            fac = sb.tile([P, npc], F32, name=f"fac{m}")
-            terms = sb.tile([P, npc], F32, name=f"terms{m}")
-            total = sb.tile([P, 1], F32, name=f"total{m}")
-            inv = sb.tile([P, 1], F32, name=f"inv{m}")
             res = sb.tile([P, T], F32, name=f"res{m}")
-            nc.vector.tensor_reduce(nall[:], nmax[m][:], AX.X, ALU.min)
-            nc.scalar.activation(fac[:], nmax[m][:], ACT.Exp, bias=nall[:], scale=-1.0)
-            nc.vector.scalar_tensor_tensor(terms[:], fac[:], 1.0 / 512.0, sums[m][:], ALU.mult, ALU.mult, accum_out=total[:])
-            nc.vector.reciprocal(inv[:], total[:])
-            for k, (c0, n, tags) in enumerate(pieces):
+            for k, (c0, n, tag) in enumerate(pieces[m]):
                 cols = slice(c0 * CH, (c0 + n) * CH)
-                nc.vector.tensor_scalar(res[:, cols], ex[m][:, cols], fac[:, k:k + 1], inv[:], ALU.mult, ALU.mult)
+                nc.vector.tensor_scalar(res[:, cols], ex[m][:, cols], fac[m][:, k:k + 1], inv[m][:], ALU.mult, ALU.mult)
                 if (c0 + n) % 2 == 0:
                     half = slice((c0 + n) * CH - HALF, (c0 + n) * CH)
                     nc.sync.dma_start(out[m * P:(m + 1) * P, half], res[:, half])

@@ -52,12 +52,10 @@ def tile_attend_turnedkeys_kernel(tc, query_words, query_scales, keys, cosn, sin
         qs = sb.tile([P, V], U8, name="qs")
         ident = sb.tile([P, P], F32, name="ident")
 
-        for r in range(2):
+        for r in range(4):
             nc.vector.memset(kf_t[r][:].bitcast(I32), 0)
         make_identity(nc, ident[:])
         nc.gpsimd.memset(qs[:].bitcast(I32), 0)
-        for r in range(2, 4):
-            nc.gpsimd.memset(kf_t[r][:].bitcast(I32), 0)
 
         nc.sync.dma_start(o_dist[:], offs3)
         nc.sync.dma_start(cos_t[0][:], cos_r[:, 0, :])

from contextlib import ExitStack

import concourse.mybir as mybir
from concourse.masks import make_identity

D, T, I, U, V, Q = 512, 1024, 256, 512, 1024, 256
FLOPS = 2 * Q * T * D

F32 = mybir.dt.float32
BF16 = mybir.dt.bfloat16
I32 = mybir.dt.int32
U32 = mybir.dt.uint32
U16 = mybir.dt.uint16
U8 = mybir.dt.uint8
FP8X4 = mybir.dt.float8_e4m3fn_x4
ALU = mybir.AluOpType
ACT = mybir.ActivationFunctionType
AX = mybir.AxisListType

P = 128
CH = 256
NCH = T // CH
HALF = 512


def tile_attend_turnedkeys_kernel(tc, query_words, query_scales, keys, cosn, sinn, kept, offs, offs2, offs3, offs4, out):
    nc = tc.nc
    with ExitStack() as ctx:
        lists = ctx.enter_context(tc.tile_pool(name="lists", bufs=1))
        sb = ctx.enter_context(tc.tile_pool(name="sb", bufs=1))
        ps = ctx.enter_context(tc.psum_pool(name="ps", bufs=1))

        o_key = lists.tile([P, I // 16], U16, name="o_key")
        o_place = lists.tile([P, I // 16], U16, name="o_place")
        o_dist = lists.tile([P, I // 16], U16, name="o_dist")
        o_query = lists.tile([P, Q // 16], U16, name="o_query")

        keys_r = keys.rearrange("(p r) t -> p r t", r=4)
        kept_r = kept.rearrange("(p r) t -> p r t", r=4)
        cos_r = cosn.rearrange("(p r) u -> p r u", r=4)
        sin_r = sinn.rearrange("(p r) u -> p r u", r=4)

        key0 = sb.tile([P, T], F32, name="key0")
        key1 = sb.tile([P, T], F32, name="key1")
        key23 = sb.tile([P, 2 * T], F32, name="key23")
        key_w = [key0[:], key1[:], key23[:, 0:T], key23[:, T:2 * T]]
        kept_t = [sb.tile([P, T], F32, name=f"kept{r}") for r in range(4)]
        kf_t = [sb.tile([P, T], F32, name=f"kf{r}") for r in range(4)]
        cos_t = [sb.tile([P, U], F32, name=f"cos{u}") for u in range(2)]
        sin_t = [sb.tile([P, U], F32, name=f"sin{u}") for u in range(2)]
        qw = sb.tile([P, V], U32, name="qw")
        qs = sb.tile([P, V], U8, name="qs")
        ident = sb.tile([P, P], F32, name="ident")

        for r in range(4):
            nc.vector.memset(kf_t[r][:].bitcast(I32), 0)
        make_identity(nc, ident[:])
        nc.gpsimd.memset(qs[:].bitcast(I32), 0)

        nc.sync.dma_start(o_dist[:], offs3)
        nc.sync.dma_start(cos_t[0][:], cos_r[:, 0, :])
        nc.sync.dma_start(sin_t[0][:], sin_r[:, 0, :])
        nc.sync.dma_start(o_key[:], offs)
        nc.sync.dma_start(key0[:], keys_r[:, 0, :])
        nc.sync.dma_start(cos_t[1][:], cos_r[:, 2, :])
        nc.sync.dma_start(key1[:], keys_r[:, 1, :])
        nc.sync.dma_start(sin_t[1][:], sin_r[:, 2, :])
        nc.sync.dma_start(o_place[:], offs2)
        nc.sync.dma_start(kept_t[0][:], kept_r[:, 0, :])
        nc.sync.dma_start(kept_t[1][:], kept_r[:, 1, :])
        nc.sync.dma_start(key23[:], keys.rearrange("(p g r) t -> p g (r t)", g=2, r=2)[:, 1, :])
        nc.sync.dma_start(kept_t[2][:], kept_r[:, 2, :])
        nc.sync.dma_start(kept_t[3][:], kept_r[:, 3, :])
        nc.sync.dma_start(qw[:].bitcast(I32), query_words[0].rearrange("p n t -> p (n t)").bitcast(I32))
        nc.sync.dma_start(o_query[:], offs4)
        qs_rows = query_scales[0].bitcast(I32)
        for g in range(4):
            nc.sync.dma_start(qs[:].bitcast(I32)[32 * g:32 * g + 4, :], qs_rows[4 * g:4 * g + 4, :])

        qwg = sb.tile([P, Q], U32, name="qwg", align_bytes=64)
        qsg = sb.tile([P, Q], U8, name="qsg", align_bytes=64)

        def rotate_and_scatter(u):
            trig = sb.tile([P, 3, I], F32, name=f"trig{u}")
            kg = [sb.tile([P, I], F32, name=f"kg{u}_{e}") for e in range(2)]
            prod = [sb.tile([P, 2, I], F32, name=f"prod{u}_{e}") for e in range(2)]
            nc.vector.tensor_copy(trig[:, 1, :], cos_t[u][:].indirect(o_dist[:]))
            nc.vector.tensor_copy(trig[:, 0, :], sin_t[u][:].indirect(o_dist[:]))
            nc.scalar.mul(trig[:, 2, :], trig[:, 0, :], -1.0)
            for e in range(2):
                nc.vector.tensor_copy(kg[e][:], key_w[2 * u + e].indirect(o_key[:]))
            for e in range(2):
                nc.vector.tensor_tensor(prod[e][:], kg[e][:].unsqueeze(1).to_broadcast([P, 2, I]), trig[:, e:e + 2, :], ALU.mult)
            for e in range(2):
                nc.vector.tensor_tensor(kf_t[2 * u + e][:].indirect(o_place[:]), prod[0][:, 1 - e, :], prod[1][:, 1 - e, :], ALU.add)

        def add_turned(u, banks):
            for src, first in ((kept_t, True), (kf_t, False)):
                for e in range(2):
                    for c in range(NCH):
                        for j in range(2):
                            t0 = c * CH + j * P
                            nc.tensor.matmul(
                                banks[c][:, j, e, :], src[2 * u + e][:, t0:t0 + P], ident[:],
                                start=(first and e == 0 and j == 0),
                                stop=((not first) and e == 1 and j == 1),
                                is_transpose=True,
                            )

        def round_pairs(u, c, bank, on_vector):
            w = sb.tile([P, 2, P, 2], BF16, name=f"w{u}_{c}")
            src = bank[:].rearrange("t j e p -> t j p e")
            if on_vector:
                nc.vector.tensor_copy(w[:], src)
            else:
                nc.scalar.copy(w[:], src)
            return w

        def turn_back(u, w, bank):
            words = w[:].rearrange("t j p e -> t (j p e)").bitcast(F32)
            for j in range(2):
                nc.tensor.transpose(bank[:, u, j * P:(j + 1) * P], words[:, j * P:(j + 1) * P], ident[:])

        banks0 = [ps.tile([P, 2, 2, P], F32, name=f"sum0_{c}", tag=f"a{c}") for c in range(NCH)]
        banks1 = [ps.tile([P, 2, 2, P], F32, name=f"sum1_{c}", tag=f"b{c}") for c in range(NCH)]

        rotate_and_scatter(0)
        add_turned(0, banks0)
        w0 = [round_pairs(0, c, banks0[c], False) for c in range(NCH)]
        back = [ps.tile([P, 2, CH], F32, name=f"back{c}", tag=f"a{c}") for c in range(NCH)]
        rotate_and_scatter(1)
        nc.vector.tensor_copy(qwg[:], qw[:].indirect(o_query[:]))
        nc.vector.tensor_copy(qsg[:], qs[:].indirect(o_query[:]))
        for c in range(NCH):
            turn_back(0, w0[c], back[c])
        add_turned(1, banks1)
        w1 = [round_pairs(1, c, banks1[c], c >= 2) for c in range(NCH)]
        for c in range(NCH):
            turn_back(1, w1[c], back[c])

        pieces = [
            [(0, 1, "b0"), (1, 1, "b2"), (2, 1, "a0"), (3, 1, "a2")],
            [(0, 2, "b1"), (2, 1, "a1"), (3, 1, "a3")],
        ]
        nmax = [sb.tile([P, len(pieces[m])], F32, name=f"nmax{m}") for m in range(2)]
        sums = [sb.tile([P, len(pieces[m])], F32, name=f"sums{m}") for m in range(2)]
        ex = [sb.tile([P, T], F32, name=f"ex{m}") for m in range(2)]
        quant = []
        for c in range(NCH):
            knb = sb.tile([P, CH * 4], BF16, name=f"knb{c}", align_bytes=64)
            dst = knb[:].bitcast(F32).rearrange("p (t u) -> p t u", u=2)
            src = back[c][:].rearrange("p u t -> p t u")
            nc.scalar.copy(dst, src)
            codes = sb.tile([P, CH], U32, name=f"codes{c}", align_bytes=64)
            scales = sb.tile([P, CH], U8, name=f"scales{c}", align_bytes=64)
            nc.vector.quantize_mx(out=codes[:].bitcast(FP8X4), scales=scales[:], in_=knb[:])
            quant.append((codes, scales))

        score = [[ps.tile([P, n * CH], F32, name=f"score{m}_{c0}", tag=tag) for c0, n, tag in pieces[m]] for m in range(2)]
        for c in range(NCH):
            for m in range(2):
                for k, (c0, n, tag) in enumerate(pieces[m]):
                    if c0 <= c < c0 + n:
                        nc.tensor.matmul_mx(
                            out=score[m][k][:, (c - c0) * CH:(c - c0 + 1) * CH],
                            lhsT=qwg[:, m * P:(m + 1) * P].bitcast(FP8X4),
                            lhsT_scale=qsg[:, m * P:(m + 1) * P],
                            rhs=quant[c][0][:].bitcast(FP8X4),
                            rhs_scale=quant[c][1][:],
                            start=True, stop=True,
                        )

        fac = [sb.tile([P, len(pieces[m])], F32, name=f"fac{m}") for m in range(2)]
        inv = [sb.tile([P, 1], F32, name=f"inv{m}") for m in range(2)]
        for m in range(2):
            for k, (c0, n, tag) in enumerate(pieces[m]):
                nc.vector.tensor_reduce(nmax[m][:, k:k + 1], score[m][k][:], AX.X, ALU.max, negate=True)
                nc.scalar.activation(ex[m][:, c0 * CH:(c0 + n) * CH], score[m][k][:], ACT.Exp, bias=nmax[m][:, k:k + 1], accum_out=sums[m][:, k:k + 1])
            nall = sb.tile([P, 1], F32, name=f"nall{m}")
            terms = sb.tile([P, len(pieces[m])], F32, name=f"terms{m}")
            total = sb.tile([P, 1], F32, name=f"total{m}")
            nc.vector.tensor_reduce(nall[:], nmax[m][:], AX.X, ALU.min)
            nc.scalar.activation(fac[m][:], nmax[m][:], ACT.Exp, bias=nall[:], scale=-1.0)
            nc.vector.scalar_tensor_tensor(terms[:], fac[m][:], 1.0 / 512.0, sums[m][:], ALU.mult, ALU.mult, accum_out=total[:])
            nc.vector.reciprocal(inv[m][:], total[:])

        for m in range(2):
            res = sb.tile([P, T], F32, name=f"res{m}")
            for k, (c0, n, tag) in enumerate(pieces[m]):
                cols = slice(c0 * CH, (c0 + n) * CH)
                nc.vector.tensor_scalar(res[:, cols], ex[m][:, cols], fac[m][:, k:k + 1], inv[m][:], ALU.mult, ALU.mult)
                if (c0 + n) % 2 == 0:
                    half = slice((c0 + n) * CH - HALF, (c0 + n) * CH)
                    nc.sync.dma_start(out[m * P:(m + 1) * P, half], res[:, half])
